import numpy as np
import ml_dtypes


def mxq(x, axis, fmt="e4m3"):
    dtype, down = {"e4m3": (ml_dtypes.float8_e4m3fn, 7), "e5m2": (ml_dtypes.float8_e5m2, 14)}[fmt]
    v = np.moveaxis(np.asarray(x, np.float32).astype(ml_dtypes.bfloat16).astype(np.float64), axis, -1)
    blocks = v.reshape(v.shape[:-1] + (-1, 32))
    amax = np.abs(blocks).max(-1, keepdims=True)
    byte = np.maximum(np.where(amax > 0, np.frexp(amax)[1] - 1 + 127, 0) - down, 1)
    scale = np.exp2(byte - 127.0)
    codes = (blocks / scale).astype(np.float32).astype(dtype).astype(np.float64)
    return np.moveaxis((codes * scale).reshape(v.shape), -1, axis)


WIDE = False


def mx_kscale(k):
    if not WIDE:
        return np.ones(k)
    levels = np.array([10, -10, 5, -5, 0])
    if k % 512:
        return np.exp2(np.random.permutation(np.resize(levels, k // 32))).repeat(32)
    a = np.empty((k // 512, 16))
    for p in range(k // 512):
        a[p, :8] = np.random.permutation(np.resize(levels, 8))
        for g in range(8):
            far = levels[np.abs(levels - a[p, g]) >= 10]
            a[p, g + 8] = far[np.random.randint(len(far))]
    return np.exp2(a.ravel()).repeat(32)


def f64(x):
    return np.asarray(x).astype(np.float64)


def striped(idx):
    return np.tile(idx.reshape(-1, 16).T, (8, 1)).astype(np.uint16)


def unstriped(offs):
    return offs[:16].T.reshape(-1).astype(np.int64)


def striped8(idx):
    return np.concatenate([x.reshape(-1, 16).T for x in idx]).astype(np.uint16)


def runs(offs, k):
    lists = np.stack([offs[16 * r : 16 * r + 16].T.reshape(-1) for r in range(8)]).astype(np.int64)
    return lists[np.arange(k) % 512 // 64]


def pack_weight(w):
    k, n = w.shape
    w = f64(np.asarray(w, np.float32).astype(ml_dtypes.bfloat16)).reshape(k // 32, 32, n)
    amax = np.abs(w).max(1)
    byte = np.clip(np.where(amax > 0, np.frexp(amax)[1] - 1 + 127 - 7, 1), 1, 254)
    scaled = (w * np.exp2(127.0 - byte)[:, None, :]).reshape(k, n).astype(np.float32)
    words = np.ascontiguousarray(scaled.reshape(k // 512, 128, 4, n).transpose(0, 1, 3, 2)).astype(ml_dtypes.float8_e4m3fn).view(np.uint8)
    return words, np.ascontiguousarray(byte.astype(np.uint8).reshape(k // 512, 16, n))


def unpack_weight(words, scales):
    g, p, n, _ = words.shape
    vals = np.ascontiguousarray(words).view(ml_dtypes.float8_e4m3fn).astype(np.float64) * np.repeat(np.exp2(scales.astype(np.float64) - 127.0), 8, axis=1)[..., None]
    return vals.transpose(0, 1, 3, 2).reshape(g * 512, n)


def sigmoid(v):
    return 1.0 / (1.0 + np.exp(-np.maximum(v, -700.0)))


K, T, S, G, H, W = 512, 2048, 512, 2048, 512, 384


def setup_inputs():
    n = np.random.standard_normal
    s = mx_kscale(K)[:, None]
    packed_xT = pack_weight(n((K, T)) * s)
    packed_dT = pack_weight(n((K, G)) / s)
    return {
        "x_words": packed_xT[0],
        "x_scales": packed_xT[1],
        "d_words": packed_dT[0],
        "d_scales": packed_dT[1],
        "gs": (np.random.uniform(0.5, 1.5, (K, 1)) * s).astype(np.float32),
        "offs": striped(np.random.permutation(T)[:S]),
        "k1": striped8(np.random.randint(0, G, (8, H))),
        "n1": striped(np.random.permutation(S)),
        "n2": striped(np.random.permutation(S)),
        "n3": striped(np.random.permutation(S)[:W]),
        "n4": striped(np.random.permutation(S)[:W]),
    }


def reference(x_words, x_scales, d_words, d_scales, gs, offs, k1, n1, n2, n3, n4):
    d_k1 = unpack_weight(d_words, d_scales)[np.arange(K)[:, None], runs(k1, K)]
    xq = unpack_weight(x_words, x_scales)[:, unstriped(offs)]
    h = 0.0625 * (d_k1.T @ xq)
    st = h[:, unstriped(n1)] - h
    z = f64(gs) * (h * (sigmoid(st[:, unstriped(n2)])))
    h2 = 0.0625 * ((d_k1.T @ mxq(z, 0, "e4m3")))
    old = h2[:, unstriped(n3)]
    pa = h2[:, unstriped(n4)]
    ra = old - np.tanh(pa)
    out = h2.copy()
    out[:, unstriped(n3)] = ra
    return out

@@ -1,0 +1,181 @@
+from contextlib import ExitStack
+
+import concourse.mybir as mybir
+
+F32 = mybir.dt.float32
+BF16 = mybir.dt.bfloat16
+I32 = mybir.dt.int32
+U32 = mybir.dt.uint32
+U16 = mybir.dt.uint16
+U8 = mybir.dt.uint8
+FP8X4 = mybir.dt.float8_e4m3fn_x4
+ACT = mybir.ActivationFunctionType
+ALU = mybir.AluOpType
+
+P = 128
+PACK = 4
+K = 512
+S = 512
+T = 2048
+W = 384
+HALF = S // 2
+SIXTEENTH = 0.0625
+CHUNK = 128
+EARLY = S - CHUNK
+
+FLOPS = 2 * 2 * K * K * S
+
+
+def entries(lst, start, count):
+    return lst[:, start // 16 : (start + count) // 16]
+
+
+def tile_picked_ringhopdktanh_none_p_kernel(
+    tc, x_words, x_scales, d_words, d_scales, gs, offs, k1, n1, n2, n3, n4, out
+):
+    nc = tc.nc
+    with ExitStack() as ctx:
+        keep = ctx.enter_context(tc.tile_pool(name="keep", bufs=1))
+        psum = ctx.enter_context(tc.psum_pool(name="psum", bufs=8))
+
+        def load_list(ap, name):
+            tile = keep.tile(list(ap.shape), U16, name=name)
+            nc.sync.dma_start(tile[:], ap)
+            return tile
+
+        d_bytes_all = keep.tile([P, T], U8, name="d_bytes_all")
+        x_bytes_all = keep.tile([P, T], U8, name="x_bytes_all")
+        d_words_all = keep.tile([P, T], I32, name="d_words_all")
+        x_words_all = keep.tile([P, T], I32, name="x_words_all")
+        nc.vector.memset(d_bytes_all[:].bitcast(I32), 0)
+        nc.vector.memset(x_bytes_all[:].bitcast(I32), 0)
+
+        k1_t = load_list(k1, "k1_t")
+        offs_t = load_list(offs, "offs_t")
+        nc.sync.dma_start(d_bytes_all[0:P:8, :].bitcast(I32), d_scales[0].bitcast(I32))
+        nc.sync.dma_start(d_words_all[:], d_words[0].rearrange("p n t -> p (n t)").bitcast(I32))
+        for q in range(4):
+            nc.scalar.dma_start(
+                x_bytes_all[32 * q : 32 * q + 4, :].bitcast(I32), x_scales[0, 4 * q : 4 * q + 4, :].bitcast(I32)
+            )
+        nc.sync.dma_start(x_words_all[:], x_words[0].rearrange("p n t -> p (n t)").bitcast(I32))
+        n1_t = load_list(n1, "n1_t")
+        n2_t = load_list(n2, "n2_t")
+        n3_t = load_list(n3, "n3_t")
+        n4_t = load_list(n4, "n4_t")
+        gain = keep.tile([P, PACK], F32, name="gain")
+        nc.gpsimd.dma_start(gain[:], gs.rearrange("(p t) o -> p (t o)", t=PACK))
+
+        d_bytes = keep.tile([P, K], U8, name="d_bytes", tag="picked", align_bytes=64)
+        nc.vector.tensor_copy(d_bytes[:], d_bytes_all[:].indirect(k1_t[:]))
+        d_plane = keep.tile([P, K], U8, name="d_plane", align_bytes=64)
+        nc.vector.tensor_copy(
+            d_plane[:].rearrange("p (t m) -> p m t", t=PACK), d_bytes[:].rearrange("p (m t) -> p m t", t=PACK)
+        )
+        for j in range(1, 4):
+            nc.scalar.dma_start(d_plane[j:P:32, :].bitcast(I32), d_plane[8 * j : P : 32, :].bitcast(I32))
+
+        x_plane = keep.tile([P, S], U8, name="x_plane", align_bytes=64)
+        nc.vector.tensor_copy(x_plane[:], x_bytes_all[:].indirect(offs_t[:]))
+
+        d_picked = keep.tile([P, K], U32, name="d_picked", tag="picked", align_bytes=64)
+        nc.vector.tensor_copy(d_picked[:], d_words_all[:].bitcast(U32).indirect(k1_t[:]))
+        d_codes = keep.tile([P, K], U32, name="d_codes", align_bytes=64)
+        nc.vector.tensor_copy(
+            d_codes[:].rearrange("p (t c i) -> p c t i", t=PACK, i=4),
+            d_picked[:].rearrange("p (c i t) -> p c t i", t=PACK, i=4),
+        )
+
+        def product(acc, t, codes, plane):
+            rows = slice(P * t, P * (t + 1))
+            nc.tensor.matmul_mx(
+                out=acc,
+                lhsT=d_codes[:, rows].bitcast(FP8X4),
+                lhsT_scale=d_plane[:, rows],
+                rhs=codes.bitcast(FP8X4),
+                rhs_scale=plane,
+                start=True,
+                stop=True,
+            )
+
+        x_codes = keep.tile([P, S], U32, name="x_codes", align_bytes=64)
+        h = [keep.tile([P, S], F32, name=f"h{t}") for t in range(PACK)]
+        halves = [slice(0, HALF), slice(HALF, S)]
+        for cols in halves:
+            nc.vector.tensor_copy(
+                x_codes[:, cols], x_words_all[:].bitcast(U32).indirect(entries(offs_t, cols.start, HALF))
+            )
+        for t in range(PACK):
+            for cols in halves:
+                acc = psum.tile([P, HALF], F32, name="acc", tag="acc")
+                product(acc[:], t, x_codes[:, cols], x_plane[:, cols])
+                if cols.start == 0 and t < 2:
+                    nc.scalar.activation(h[t][:, cols], acc[:], ACT.Copy, scale=SIXTEENTH)
+                else:
+                    nc.vector.tensor_scalar(h[t][:, cols], acc[:], SIXTEENTH, None, ALU.mult)
+
+        st = [keep.tile([P, S], F32, name=f"st{t}") for t in range(PACK)]
+        weighted = keep.tile([P, PACK, S], F32, name="weighted")
+        for t in range(PACK):
+            nc.vector.tensor_scalar(weighted[:, t, :], h[t][:], gain[:, t : t + 1], None, ALU.mult)
+            hop = keep.tile([P, S], F32, name=f"hop{t}", tag=f"hop{t}")
+            for half in range(2):
+                cols = slice(HALF * half, HALF * (half + 1))
+                nc.scalar.activation(hop[:, cols], h[t][:].indirect(entries(n1_t, HALF * half, HALF)), ACT.Copy)
+            nc.vector.tensor_tensor(st[t][:], hop[:], h[t][:], ALU.subtract)
+
+        h2 = [keep.tile([P, S], F32, name=f"h2_{t}") for t in range(PACK)]
+        neg_tanh = [keep.tile([P, S], F32, name=f"neg_tanh{t}") for t in range(PACK)]
+        early = [psum.tile([P, EARLY], F32, name="acc", tag="acc") for t in range(PACK)]
+        late = [psum.tile([P, CHUNK], F32, name="acc", tag="acc") for t in range(PACK)]
+
+        def leave_bank(t, bank, cols):
+            nc.vector.tensor_scalar(h2[t][:, cols], bank[:], SIXTEENTH, None, ALU.mult)
+
+        def tanh_of_bank(t, bank, cols):
+            nc.scalar.activation(neg_tanh[t][:, cols], bank[:], ACT.Tanh, scale=-SIXTEENTH)
+
+        first_gate = keep.tile([P, PACK, CHUNK], F32, name="first_gate", tag=f"hop{PACK - 2}")
+        later_gates = keep.tile([P, S // CHUNK - 1, PACK, CHUNK], F32, name="later_gates", tag=f"hop{PACK - 1}")
+        for start in range(0, S, CHUNK):
+            gate = first_gate[:] if start == 0 else later_gates[:, start // CHUNK - 1]
+            for t in range(PACK):
+                nc.scalar.activation(gate[:, t, :], st[t][:].indirect(entries(n2_t, start, CHUNK)), ACT.Sigmoid)
+            z = keep.tile([P, CHUNK, PACK], BF16, name=f"z{start}", align_bytes=64)
+            nc.vector.tensor_tensor(
+                z[:].rearrange("p (c i) t -> p c t i", i=4),
+                weighted[:, :, start : start + CHUNK].rearrange("p t (c i) -> p c t i", i=4),
+                gate.rearrange("p t (c i) -> p c t i", i=4),
+                ALU.mult,
+            )
+            z_codes = keep.tile([P, CHUNK], U32, name=f"z_codes{start}", align_bytes=64)
+            z_plane = keep.tile([P, CHUNK], U8, name=f"z_plane{start}", align_bytes=64)
+            nc.vector.quantize_mx(
+                out=z_codes[:].bitcast(FP8X4), scales=z_plane[:], in_=z[:].rearrange("p c t -> p (c t)")
+            )
+            for t in range(PACK):
+                acc = early[t][:, start : start + CHUNK] if start < EARLY else late[t][:]
+                product(acc, t, z_codes[:], z_plane[:])
+        for t in range(PACK):
+            tanh_of_bank(t, early[t], slice(0, EARLY))
+
+        out_rows = out.rearrange("(p t) j -> t p j", t=PACK)
+        ra = [keep.tile([P, W], F32, name=f"ra{t}") for t in range(PACK)]
+
+        def fetch(t):
+            leave_bank(t, early[t], slice(0, EARLY))
+            leave_bank(t, late[t], slice(EARLY, S))
+            tanh_of_bank(t, late[t], slice(EARLY, S))
+            old = keep.tile([P, W], F32, name=f"old{t}")
+            nc.scalar.activation(old[:], h2[t][:].indirect(n3_t[:]), ACT.Copy)
+            nc.vector.tensor_tensor(ra[t][:], neg_tanh[t][:].indirect(n4_t[:]), old[:], ALU.add)
+
+        def put(t):
+            nc.scalar.activation(h2[t][:].indirect(n3_t[:]), ra[t][:], ACT.Copy)
+            nc.sync.dma_start(out_rows[t], h2[t][:])
+
+        fetch(0)
+        for t in range(1, PACK):
+            fetch(t)
+            put(t - 1)
+        put(PACK - 1)

@@ -65,6 +65,8 @@ def tile_picked_ringhopdktanh_none_p_kernel(
         n4_t = load_list(n4, "n4_t")
         gain = keep.tile([P, PACK], F32, name="gain")
         nc.gpsimd.dma_start(gain[:], gs.rearrange("(p t) o -> p (t o)", t=PACK))
+        warm = keep.tile([P, 1], F32, name="warm")
+        nc.scalar.activation(warm[:], gain[:, 0:1], ACT.Sigmoid)
 
         d_bytes = keep.tile([P, K], U8, name="d_bytes", tag="picked", align_bytes=64)
         nc.vector.tensor_copy(d_bytes[:], d_bytes_all[:].indirect(k1_t[:]))

@@ -20,6 +20,7 @@ T = 2048
 W = 384
 HALF = S // 2
 SIXTEENTH = 0.0625
+SPARE = 8
 CHUNK = 128
 EARLY = S - CHUNK
 
@@ -51,11 +52,12 @@ def tile_picked_ringhopdktanh_none_p_kernel(
         nc.vector.memset(x_bytes_all[:].bitcast(I32), 0)
 
         k1_t = load_list(k1, "k1_t")
+        for e in range(2):
+            nc.scalar.dma_start(d_bytes_all[e:P:16, :].bitcast(I32), d_scales[0, e:16:2, :].bitcast(I32))
         offs_t = load_list(offs, "offs_t")
-        nc.sync.dma_start(d_bytes_all[0:P:8, :].bitcast(I32), d_scales[0].bitcast(I32))
         nc.sync.dma_start(d_words_all[:], d_words[0].rearrange("p n t -> p (n t)").bitcast(I32))
         for q in range(4):
-            nc.scalar.dma_start(
+            nc.sync.dma_start(
                 x_bytes_all[32 * q : 32 * q + 4, :].bitcast(I32), x_scales[0, 4 * q : 4 * q + 4, :].bitcast(I32)
             )
         nc.sync.dma_start(x_words_all[:], x_words[0].rearrange("p n t -> p (n t)").bitcast(I32))
@@ -72,13 +74,10 @@ def tile_picked_ringhopdktanh_none_p_kernel(
         nc.vector.tensor_copy(d_bytes[:], d_bytes_all[:].indirect(k1_t[:]))
         d_plane = keep.tile([P, K], U8, name="d_plane", align_bytes=64)
         nc.vector.tensor_copy(
-            d_plane[:].rearrange("p (t m) -> p m t", t=PACK), d_bytes[:].rearrange("p (m t) -> p m t", t=PACK)
+            d_plane[:].rearrange("p (t m) -> p t m", t=PACK), d_bytes[:].rearrange("p (m t) -> p t m", t=PACK)
         )
-        for j in range(1, 4):
-            nc.scalar.dma_start(d_plane[j:P:32, :].bitcast(I32), d_plane[8 * j : P : 32, :].bitcast(I32))
-
-        x_plane = keep.tile([P, S], U8, name="x_plane", align_bytes=64)
-        nc.vector.tensor_copy(x_plane[:], x_bytes_all[:].indirect(offs_t[:]))
+        for e in range(2):
+            nc.scalar.dma_start(d_plane[2 + e : P : 32, :].bitcast(I32), d_plane[16 + e : P : 32, :].bitcast(I32))
 
         d_picked = keep.tile([P, K], U32, name="d_picked", tag="picked", align_bytes=64)
         nc.vector.tensor_copy(d_picked[:], d_words_all[:].bitcast(U32).indirect(k1_t[:]))
@@ -87,6 +86,9 @@ def tile_picked_ringhopdktanh_none_p_kernel(
             d_codes[:].rearrange("p (t c i) -> p c t i", t=PACK, i=4),
             d_picked[:].rearrange("p (c i t) -> p c t i", t=PACK, i=4),
         )
+
+        x_plane = keep.tile([P, S], U8, name="x_plane", align_bytes=64)
+        nc.vector.tensor_copy(x_plane[:], x_bytes_all[:].indirect(offs_t[:]))
 
         def product(acc, t, codes, plane):
             rows = slice(P * t, P * (t + 1))
@@ -101,7 +103,9 @@ def tile_picked_ringhopdktanh_none_p_kernel(
             )
 
         x_codes = keep.tile([P, S], U32, name="x_codes", align_bytes=64)
-        h = [keep.tile([P, S], F32, name=f"h{t}") for t in range(PACK)]
+        h = [keep.tile([P, S + SPARE], F32, name=f"h{t}") for t in range(PACK)]
+        for t in range(PACK):
+            nc.gpsimd.memset(h[t][:, S:], 0.0)
         halves = [slice(0, HALF), slice(HALF, S)]
         for cols in halves:
             nc.vector.tensor_copy(
@@ -119,12 +123,10 @@ def tile_picked_ringhopdktanh_none_p_kernel(
         st = [keep.tile([P, S], F32, name=f"st{t}") for t in range(PACK)]
         weighted = keep.tile([P, PACK, S], F32, name="weighted")
         for t in range(PACK):
-            nc.vector.tensor_scalar(weighted[:, t, :], h[t][:], gain[:, t : t + 1], None, ALU.mult)
+            nc.vector.tensor_scalar(weighted[:, t, :], h[t][:, :S], gain[:, t : t + 1], None, ALU.mult)
             hop = keep.tile([P, S], F32, name=f"hop{t}", tag=f"hop{t}")
-            for half in range(2):
-                cols = slice(HALF * half, HALF * (half + 1))
-                nc.scalar.activation(hop[:, cols], h[t][:].indirect(entries(n1_t, HALF * half, HALF)), ACT.Copy)
-            nc.vector.tensor_tensor(st[t][:], hop[:], h[t][:], ALU.subtract)
+            nc.scalar.activation(hop[:], h[t][:].indirect(n1_t[:]), ACT.Copy)
+            nc.vector.tensor_tensor(st[t][:], hop[:], h[t][:, :S], ALU.subtract)
 
         h2 = [keep.tile([P, S], F32, name=f"h2_{t}") for t in range(PACK)]
         neg_tanh = [keep.tile([P, S], F32, name=f"neg_tanh{t}") for t in range(PACK)]
@@ -145,9 +147,9 @@ def tile_picked_ringhopdktanh_none_p_kernel(
                 nc.scalar.activation(gate[:, t, :], st[t][:].indirect(entries(n2_t, start, CHUNK)), ACT.Sigmoid)
             z = keep.tile([P, CHUNK, PACK], BF16, name=f"z{start}", align_bytes=64)
             nc.vector.tensor_tensor(
-                z[:].rearrange("p (c i) t -> p c t i", i=4),
-                weighted[:, :, start : start + CHUNK].rearrange("p t (c i) -> p c t i", i=4),
-                gate.rearrange("p t (c i) -> p c t i", i=4),
+                z[:].rearrange("p (c i) t -> p c t i", i=2),
+                weighted[:, :, start : start + CHUNK].rearrange("p t (c i) -> p c t i", i=2),
+                gate.rearrange("p t (c i) -> p c t i", i=2),
                 ALU.mult,
             )
             z_codes = keep.tile([P, CHUNK], U32, name=f"z_codes{start}", align_bytes=64)

@@ -56,10 +56,14 @@ def tile_picked_ringhopdktanh_none_p_kernel(
             nc.scalar.dma_start(d_bytes_all[e:P:16, :].bitcast(I32), d_scales[0, e:16:2, :].bitcast(I32))
         offs_t = load_list(offs, "offs_t")
         nc.sync.dma_start(d_words_all[:], d_words[0].rearrange("p n t -> p (n t)").bitcast(I32))
-        for q in range(4):
-            nc.sync.dma_start(
+
+        def load_x_scale_rows(queue, q):
+            queue.dma_start(
                 x_bytes_all[32 * q : 32 * q + 4, :].bitcast(I32), x_scales[0, 4 * q : 4 * q + 4, :].bitcast(I32)
             )
+
+        for q in (0, 1):
+            load_x_scale_rows(nc.sync, q)
         nc.sync.dma_start(x_words_all[:], x_words[0].rearrange("p n t -> p (n t)").bitcast(I32))
         n1_t = load_list(n1, "n1_t")
         n2_t = load_list(n2, "n2_t")
@@ -67,10 +71,12 @@ def tile_picked_ringhopdktanh_none_p_kernel(
         n4_t = load_list(n4, "n4_t")
         gain = keep.tile([P, PACK], F32, name="gain")
         nc.gpsimd.dma_start(gain[:], gs.rearrange("(p t) o -> p (t o)", t=PACK))
+        for q in (2, 3):
+            load_x_scale_rows(nc.gpsimd, q)
         warm = keep.tile([P, 1], F32, name="warm")
         nc.scalar.activation(warm[:], gain[:, 0:1], ACT.Sigmoid)
 
-        d_bytes = keep.tile([P, K], U8, name="d_bytes", tag="picked", align_bytes=64)
+        d_bytes = keep.tile([P, K], U8, name="d_bytes", align_bytes=64)
         nc.vector.tensor_copy(d_bytes[:], d_bytes_all[:].indirect(k1_t[:]))
         d_plane = keep.tile([P, K], U8, name="d_plane", align_bytes=64)
         nc.vector.tensor_copy(
@@ -79,7 +85,7 @@ def tile_picked_ringhopdktanh_none_p_kernel(
         for e in range(2):
             nc.scalar.dma_start(d_plane[2 + e : P : 32, :].bitcast(I32), d_plane[16 + e : P : 32, :].bitcast(I32))
 
-        d_picked = keep.tile([P, K], U32, name="d_picked", tag="picked", align_bytes=64)
+        d_picked = keep.tile([P, K], U32, name="d_picked", align_bytes=64)
         nc.vector.tensor_copy(d_picked[:], d_words_all[:].bitcast(U32).indirect(k1_t[:]))
         d_codes = keep.tile([P, K], U32, name="d_codes", align_bytes=64)
         nc.vector.tensor_copy(
@@ -106,16 +112,18 @@ def tile_picked_ringhopdktanh_none_p_kernel(
         h = [keep.tile([P, S + SPARE], F32, name=f"h{t}") for t in range(PACK)]
         for t in range(PACK):
             nc.gpsimd.memset(h[t][:, S:], 0.0)
-        halves = [slice(0, HALF), slice(HALF, S)]
-        for cols in halves:
+        pieces = [slice(0, 256), slice(256, 384), slice(384, 512)]
+        for cols in pieces:
             nc.vector.tensor_copy(
-                x_codes[:, cols], x_words_all[:].bitcast(U32).indirect(entries(offs_t, cols.start, HALF))
+                x_codes[:, cols],
+                x_words_all[:].bitcast(U32).indirect(entries(offs_t, cols.start, cols.stop - cols.start)),
             )
+        cuts = [pieces, [slice(0, HALF), slice(HALF, S)], [slice(0, S)], [slice(0, S)]]
         for t in range(PACK):
-            for cols in halves:
-                acc = psum.tile([P, HALF], F32, name="acc", tag="acc")
+            for cols in cuts[t]:
+                acc = psum.tile([P, cols.stop - cols.start], F32, name="acc", tag="acc")
                 product(acc[:], t, x_codes[:, cols], x_plane[:, cols])
-                if cols.start == 0 and t < 2:
+                if cols.stop < S:
                     nc.scalar.activation(h[t][:, cols], acc[:], ACT.Copy, scale=SIXTEENTH)
                 else:
                     nc.vector.tensor_scalar(h[t][:, cols], acc[:], SIXTEENTH, None, ALU.mult)
@@ -166,20 +174,24 @@ def tile_picked_ringhopdktanh_none_p_kernel(
         out_rows = out.rearrange("(p t) j -> t p j", t=PACK)
         ra = [keep.tile([P, W], F32, name=f"ra{t}") for t in range(PACK)]
 
+        old = [keep.tile([P, W], F32, name=f"old{t}") for t in range(PACK)]
+
         def fetch(t):
             leave_bank(t, early[t], slice(0, EARLY))
             leave_bank(t, late[t], slice(EARLY, S))
             tanh_of_bank(t, late[t], slice(EARLY, S))
-            old = keep.tile([P, W], F32, name=f"old{t}")
-            nc.scalar.activation(old[:], h2[t][:].indirect(n3_t[:]), ACT.Copy)
-            nc.vector.tensor_tensor(ra[t][:], neg_tanh[t][:].indirect(n4_t[:]), old[:], ALU.add)
+            nc.scalar.activation(old[t][:], h2[t][:].indirect(n3_t[:]), ACT.Copy)
+
+        def combine(t):
+            nc.vector.tensor_tensor(ra[t][:], neg_tanh[t][:].indirect(n4_t[:]), old[t][:], ALU.add)
 
         def put(t):
             nc.scalar.activation(h2[t][:].indirect(n3_t[:]), ra[t][:], ACT.Copy)
             nc.sync.dma_start(out_rows[t], h2[t][:])
 
         fetch(0)
-        for t in range(1, PACK):
-            fetch(t)
-            put(t - 1)
-        put(PACK - 1)
+        for t in range(PACK):
+            if t + 1 < PACK:
+                fetch(t + 1)
+            combine(t)
+            put(t)

@@ -56,14 +56,10 @@ def tile_picked_ringhopdktanh_none_p_kernel(
             nc.scalar.dma_start(d_bytes_all[e:P:16, :].bitcast(I32), d_scales[0, e:16:2, :].bitcast(I32))
         offs_t = load_list(offs, "offs_t")
         nc.sync.dma_start(d_words_all[:], d_words[0].rearrange("p n t -> p (n t)").bitcast(I32))
-
-        def load_x_scale_rows(queue, q):
-            queue.dma_start(
+        for q in range(4):
+            nc.sync.dma_start(
                 x_bytes_all[32 * q : 32 * q + 4, :].bitcast(I32), x_scales[0, 4 * q : 4 * q + 4, :].bitcast(I32)
             )
-
-        for q in (0, 1):
-            load_x_scale_rows(nc.sync, q)
         nc.sync.dma_start(x_words_all[:], x_words[0].rearrange("p n t -> p (n t)").bitcast(I32))
         n1_t = load_list(n1, "n1_t")
         n2_t = load_list(n2, "n2_t")
@@ -71,8 +67,6 @@ def tile_picked_ringhopdktanh_none_p_kernel(
         n4_t = load_list(n4, "n4_t")
         gain = keep.tile([P, PACK], F32, name="gain")
         nc.gpsimd.dma_start(gain[:], gs.rearrange("(p t) o -> p (t o)", t=PACK))
-        for q in (2, 3):
-            load_x_scale_rows(nc.gpsimd, q)
         warm = keep.tile([P, 1], F32, name="warm")
         nc.scalar.activation(warm[:], gain[:, 0:1], ACT.Sigmoid)
 

from contextlib import ExitStack

import concourse.mybir as mybir

F32 = mybir.dt.float32
BF16 = mybir.dt.bfloat16
I32 = mybir.dt.int32
U32 = mybir.dt.uint32
U16 = mybir.dt.uint16
U8 = mybir.dt.uint8
FP8X4 = mybir.dt.float8_e4m3fn_x4
ACT = mybir.ActivationFunctionType
ALU = mybir.AluOpType

P = 128
PACK = 4
K = 512
S = 512
T = 2048
W = 384
HALF = S // 2
SIXTEENTH = 0.0625
SPARE = 8
CHUNK = 128
EARLY = S - CHUNK

FLOPS = 2 * 2 * K * K * S


def entries(lst, start, count):
    return lst[:, start // 16 : (start + count) // 16]


def tile_picked_ringhopdktanh_none_p_kernel(
    tc, x_words, x_scales, d_words, d_scales, gs, offs, k1, n1, n2, n3, n4, out
):
    nc = tc.nc
    with ExitStack() as ctx:
        keep = ctx.enter_context(tc.tile_pool(name="keep", bufs=1))
        psum = ctx.enter_context(tc.psum_pool(name="psum", bufs=8))

        def load_list(ap, name):
            tile = keep.tile(list(ap.shape), U16, name=name)
            nc.sync.dma_start(tile[:], ap)
            return tile

        d_bytes_all = keep.tile([P, T], U8, name="d_bytes_all")
        x_bytes_all = keep.tile([P, T], U8, name="x_bytes_all")
        d_words_all = keep.tile([P, T], I32, name="d_words_all")
        x_words_all = keep.tile([P, T], I32, name="x_words_all")
        nc.vector.memset(d_bytes_all[:].bitcast(I32), 0)
        nc.vector.memset(x_bytes_all[:].bitcast(I32), 0)

        k1_t = load_list(k1, "k1_t")
        for e in range(2):
            nc.scalar.dma_start(d_bytes_all[e:P:16, :].bitcast(I32), d_scales[0, e:16:2, :].bitcast(I32))
        offs_t = load_list(offs, "offs_t")
        nc.sync.dma_start(d_words_all[:], d_words[0].rearrange("p n t -> p (n t)").bitcast(I32))
        for q in range(4):
            nc.sync.dma_start(
                x_bytes_all[32 * q : 32 * q + 4, :].bitcast(I32), x_scales[0, 4 * q : 4 * q + 4, :].bitcast(I32)
            )
        nc.sync.dma_start(x_words_all[:], x_words[0].rearrange("p n t -> p (n t)").bitcast(I32))
        n1_t = load_list(n1, "n1_t")
        n2_t = load_list(n2, "n2_t")
        n3_t = load_list(n3, "n3_t")
        n4_t = load_list(n4, "n4_t")
        gain = keep.tile([P, PACK], F32, name="gain")
        nc.gpsimd.dma_start(gain[:], gs.rearrange("(p t) o -> p (t o)", t=PACK))
        warm = keep.tile([P, 1], F32, name="warm")
        nc.scalar.activation(warm[:], gain[:, 0:1], ACT.Sigmoid)

        d_bytes = keep.tile([P, K], U8, name="d_bytes", align_bytes=64)
        nc.vector.tensor_copy(d_bytes[:], d_bytes_all[:].indirect(k1_t[:]))
        d_plane = keep.tile([P, K], U8, name="d_plane", align_bytes=64)
        nc.vector.tensor_copy(
            d_plane[:].rearrange("p (t m) -> p t m", t=PACK), d_bytes[:].rearrange("p (m t) -> p t m", t=PACK)
        )
        for e in range(2):
            nc.scalar.dma_start(d_plane[2 + e : P : 32, :].bitcast(I32), d_plane[16 + e : P : 32, :].bitcast(I32))

        d_picked = keep.tile([P, K], U32, name="d_picked", align_bytes=64)
        nc.vector.tensor_copy(d_picked[:], d_words_all[:].bitcast(U32).indirect(k1_t[:]))
        d_codes = keep.tile([P, K], U32, name="d_codes", align_bytes=64)
        nc.vector.tensor_copy(
            d_codes[:].rearrange("p (t c i) -> p c t i", t=PACK, i=4),
            d_picked[:].rearrange("p (c i t) -> p c t i", t=PACK, i=4),
        )

        x_plane = keep.tile([P, S], U8, name="x_plane", align_bytes=64)
        nc.vector.tensor_copy(x_plane[:], x_bytes_all[:].indirect(offs_t[:]))

        def product(acc, t, codes, plane):
            rows = slice(P * t, P * (t + 1))
            nc.tensor.matmul_mx(
                out=acc,
                lhsT=d_codes[:, rows].bitcast(FP8X4),
                lhsT_scale=d_plane[:, rows],
                rhs=codes.bitcast(FP8X4),
                rhs_scale=plane,
                start=True,
                stop=True,
            )

        x_codes = keep.tile([P, S], U32, name="x_codes", align_bytes=64)
        h = [keep.tile([P, S + SPARE], F32, name=f"h{t}") for t in range(PACK)]
        for t in range(PACK):
            nc.gpsimd.memset(h[t][:, S:], 0.0)
        pieces = [slice(0, 256), slice(256, 384), slice(384, 512)]
        for cols in pieces:
            nc.vector.tensor_copy(
                x_codes[:, cols],
                x_words_all[:].bitcast(U32).indirect(entries(offs_t, cols.start, cols.stop - cols.start)),
            )
        cuts = [pieces, [slice(0, HALF), slice(HALF, S)], [slice(0, S)], [slice(0, S)]]
        for t in range(PACK):
            for cols in cuts[t]:
                acc = psum.tile([P, cols.stop - cols.start], F32, name="acc", tag="acc")
                product(acc[:], t, x_codes[:, cols], x_plane[:, cols])
                if cols.stop < S:
                    nc.scalar.activation(h[t][:, cols], acc[:], ACT.Copy, scale=SIXTEENTH)
                else:
                    nc.vector.tensor_scalar(h[t][:, cols], acc[:], SIXTEENTH, None, ALU.mult)

        st = [keep.tile([P, S], F32, name=f"st{t}") for t in range(PACK)]
        weighted = keep.tile([P, PACK, S], F32, name="weighted")
        for t in range(PACK):
            nc.vector.tensor_scalar(weighted[:, t, :], h[t][:, :S], gain[:, t : t + 1], None, ALU.mult)
            hop = keep.tile([P, S], F32, name=f"hop{t}", tag=f"hop{t}")
            nc.scalar.activation(hop[:], h[t][:].indirect(n1_t[:]), ACT.Copy)
            nc.vector.tensor_tensor(st[t][:], hop[:], h[t][:, :S], ALU.subtract)

        h2 = [keep.tile([P, S], F32, name=f"h2_{t}") for t in range(PACK)]
        neg_tanh = [keep.tile([P, S], F32, name=f"neg_tanh{t}") for t in range(PACK)]
        early = [psum.tile([P, EARLY], F32, name="acc", tag="acc") for t in range(PACK)]
        late = [psum.tile([P, CHUNK], F32, name="acc", tag="acc") for t in range(PACK)]

        def leave_bank(t, bank, cols):
            nc.vector.tensor_scalar(h2[t][:, cols], bank[:], SIXTEENTH, None, ALU.mult)

        def tanh_of_bank(t, bank, cols):
            nc.scalar.activation(neg_tanh[t][:, cols], bank[:], ACT.Tanh, scale=-SIXTEENTH)

        first_gate = keep.tile([P, PACK, CHUNK], F32, name="first_gate", tag=f"hop{PACK - 2}")
        later_gates = keep.tile([P, S // CHUNK - 1, PACK, CHUNK], F32, name="later_gates", tag=f"hop{PACK - 1}")
        for start in range(0, S, CHUNK):
            gate = first_gate[:] if start == 0 else later_gates[:, start // CHUNK - 1]
            for t in range(PACK):
                nc.scalar.activation(gate[:, t, :], st[t][:].indirect(entries(n2_t, start, CHUNK)), ACT.Sigmoid)
            z = keep.tile([P, CHUNK, PACK], BF16, name=f"z{start}", align_bytes=64)
            nc.vector.tensor_tensor(
                z[:].rearrange("p (c i) t -> p c t i", i=2),
                weighted[:, :, start : start + CHUNK].rearrange("p t (c i) -> p c t i", i=2),
                gate.rearrange("p t (c i) -> p c t i", i=2),
                ALU.mult,
            )
            z_codes = keep.tile([P, CHUNK], U32, name=f"z_codes{start}", align_bytes=64)
            z_plane = keep.tile([P, CHUNK], U8, name=f"z_plane{start}", align_bytes=64)
            nc.vector.quantize_mx(
                out=z_codes[:].bitcast(FP8X4), scales=z_plane[:], in_=z[:].rearrange("p c t -> p (c t)")
            )
            for t in range(PACK):
                acc = early[t][:, start : start + CHUNK] if start < EARLY else late[t][:]
                product(acc, t, z_codes[:], z_plane[:])
        for t in range(PACK):
            tanh_of_bank(t, early[t], slice(0, EARLY))

        out_rows = out.rearrange("(p t) j -> t p j", t=PACK)
        ra = [keep.tile([P, W], F32, name=f"ra{t}") for t in range(PACK)]

        old = [keep.tile([P, W], F32, name=f"old{t}") for t in range(PACK)]

        def fetch(t):
            leave_bank(t, early[t], slice(0, EARLY))
            leave_bank(t, late[t], slice(EARLY, S))
            tanh_of_bank(t, late[t], slice(EARLY, S))
            nc.scalar.activation(old[t][:], h2[t][:].indirect(n3_t[:]), ACT.Copy)

        def combine(t):
            nc.vector.tensor_tensor(ra[t][:], neg_tanh[t][:].indirect(n4_t[:]), old[t][:], ALU.add)

        def put(t):
            nc.scalar.activation(h2[t][:].indirect(n3_t[:]), ra[t][:], ACT.Copy)
            nc.sync.dma_start(out_rows[t], h2[t][:])

        fetch(0)
        for t in range(PACK):
            if t + 1 < PACK:
                fetch(t + 1)
            combine(t)
            put(t)
